import numpy as np
import ml_dtypes


def mxq(x, axis, fmt="e4m3"):
    dtype, down = {"e4m3": (ml_dtypes.float8_e4m3fn, 7), "e5m2": (ml_dtypes.float8_e5m2, 14)}[fmt]
    v = np.moveaxis(np.asarray(x, np.float32).astype(ml_dtypes.bfloat16).astype(np.float64), axis, -1)
    blocks = v.reshape(v.shape[:-1] + (-1, 32))
    amax = np.abs(blocks).max(-1, keepdims=True)
    byte = np.maximum(np.where(amax > 0, np.frexp(amax)[1] - 1 + 127, 0) - down, 1)
    scale = np.exp2(byte - 127.0)
    codes = (blocks / scale).astype(np.float32).astype(dtype).astype(np.float64)
    return np.moveaxis((codes * scale).reshape(v.shape), -1, axis)


WIDE = False


def mx_kscale(k):
    if not WIDE:
        return np.ones(k)
    levels = np.array([10, -10, 5, -5, 0])
    if k % 512:
        return np.exp2(np.random.permutation(np.resize(levels, k // 32))).repeat(32)
    a = np.empty((k // 512, 16))
    for p in range(k // 512):
        a[p, :8] = np.random.permutation(np.resize(levels, 8))
        for g in range(8):
            far = levels[np.abs(levels - a[p, g]) >= 10]
            a[p, g + 8] = far[np.random.randint(len(far))]
    return np.exp2(a.ravel()).repeat(32)


def f64(x):
    return np.asarray(x).astype(np.float64)


E2M1 = np.array([0.0, 0.5, 1.0, 1.5, 2.0, 3.0, 4.0, 6.0, -0.0, -0.5, -1.0, -1.5, -2.0, -3.0, -4.0, -6.0])


def pack_weight(w, fmt):
    k, n = w.shape
    w = f64(np.asarray(w, np.float32).astype(ml_dtypes.bfloat16)).reshape(k // 32, 32, n)
    amax = np.abs(w).max(1)
    if fmt == "e4m3":
        byte = np.frexp(amax)[1] - 1 + 127 - 7
    else:
        mant, ex = np.frexp(amax / 6.0)
        byte = np.where(mant > 0.5, ex, ex - 1) + 127
    byte = np.clip(np.where(amax > 0, byte, 1), 1, 254)
    scaled = (w * np.exp2(127.0 - byte)[:, None, :]).reshape(k, n).astype(np.float32)
    by_word = np.ascontiguousarray(scaled.reshape(k // 512, 128, 4, n).transpose(0, 1, 3, 2))
    if fmt == "e4m3":
        words = by_word.astype(ml_dtypes.float8_e4m3fn).view(np.uint8)
    else:
        c = by_word.astype(ml_dtypes.float4_e2m1fn).view(np.uint8) & 0xF
        words = (c[..., 0::2] | (c[..., 1::2] << 4)).reshape(k // 512, 128, 2 * n)
    return np.ascontiguousarray(words), np.ascontiguousarray(byte.astype(np.uint8).reshape(k // 512, 16, n))


def unpack_weight(words, scales, fmt):
    g, _, n = scales.shape
    words = np.ascontiguousarray(words).reshape(g, 128, n, -1)
    if fmt == "e4m3":
        vals = words.view(ml_dtypes.float8_e4m3fn).astype(np.float64)
    else:
        nib = np.empty((g, 128, n, 4), np.uint8)
        nib[..., 0::2] = words & 0xF
        nib[..., 1::2] = words >> 4
        vals = E2M1[nib]
    vals = vals * np.repeat(np.exp2(scales.astype(np.float64) - 127.0), 8, axis=1)[..., None]
    return vals.transpose(0, 1, 3, 2).reshape(g * 512, n)


K, M, T = 1024, 512, 1024


def setup_inputs():
    n = np.random.standard_normal
    s = mx_kscale(K)[:, None]
    p_w4 = pack_weight(n((K, M)) / np.sqrt(K) / s, "e2m1")
    p_w8 = pack_weight(n((K, M)) / np.sqrt(K) / s, "e4m3")
    return {
        "x": (n((K, T)) * s).astype(np.float32),
        "w4_words": p_w4[0],
        "w4_scales": p_w4[1],
        "w8_words": p_w8[0],
        "w8_scales": p_w8[1],
    }


def reference(x, w4_words, w4_scales, w8_words, w8_scales):
    xa_, xb_ = mxq(np.maximum(f64(x), 0.0), 0, "e4m3"), mxq(np.maximum(-f64(x), 0.0), 0, "e4m3")
    w4_ = unpack_weight(w4_words, w4_scales, "e2m1")
    w8_ = unpack_weight(w8_words, w8_scales, "e4m3")
    y = w4_.T @ xa_ + w8_.T @ xb_
    return y

@@ -1,0 +1,178 @@
+from contextlib import ExitStack
+
+import concourse.mybir as mybir
+
+K, M, T = 1024, 512, 1024
+FLOPS = 2 * 2 * K * M * T
+
+F32 = mybir.dt.float32
+BF16 = mybir.dt.bfloat16
+I32 = mybir.dt.int32
+U32 = mybir.dt.uint32
+U8 = mybir.dt.uint8
+FP8X4 = mybir.dt.float8_e4m3fn_x4
+FP4X4 = mybir.dt.float4_e2m1fn_x4
+ALU = mybir.AluOpType
+ACT = mybir.ActivationFunctionType
+
+P = 128
+PACK = 4
+
+
+def tile_mix_feat_fm_crelu_none_kernel(tc, x, w4_words, w4_scales, w8_words, w8_scales, out):
+    nc = tc.nc
+    with ExitStack() as ctx:
+        keep = ctx.enter_context(tc.tile_pool(name="keep", bufs=1))
+        psum = ctx.enter_context(tc.psum_pool(name="psum", bufs=1))
+        ctx.enter_context(tc.manual_schedule())
+
+        w4 = keep.tile([P, 2, 2 * M], U8, name="w4", align_bytes=64)
+        w8 = keep.tile([P, 2, 4 * M], U8, name="w8", align_bytes=64)
+        sc4 = keep.tile([P, 2, M], U8, name="sc4", align_bytes=64)
+        sc8 = keep.tile([P, M], U8, name="sc8", align_bytes=64)
+        seed = keep.tile([P, 8], F32, name="seed")
+        zero = keep.tile([P, 8], F32, name="zero")
+        raw, grouped, codes, planes, acc, res = {}, {}, {}, {}, {}, {}
+        for g in range(2):
+            for s in range(2):
+                grouped[s, g] = keep.tile([P, T, PACK], BF16, name="grp%d%d" % (s, g), align_bytes=64)
+                codes[s, g] = keep.tile([P, T], U32, name="cod%d%d" % (s, g), align_bytes=64)
+                planes[s, g] = keep.tile([P, T], U8, name="pln%d%d" % (s, g), align_bytes=64)
+        for b in range(8):
+            acc[b] = psum.tile([P, 512], F32, name="acc%d" % b)
+
+        def load_x(g, c0, c1):
+            t = keep.tile([P, PACK, c1 - c0], F32, name="raw%d_%d" % (g, c0), align_bytes=64)
+            nc.sync.dma_start(out=t[:], in_=x[512 * g : 512 * (g + 1), c0:c1].rearrange("(p j) w -> p j w", j=PACK))
+            for c in range(c0, c1, 32):
+                raw[g, c] = (t, c0)
+
+        def load_sc4(eng):
+            src = w4_scales.bitcast(I32)
+            for q in range(4):
+                eng.dma_start(
+                    out=sc4[32 * q : 32 * q + 4, :, :].bitcast(I32),
+                    in_=src[:, 4 * q : 4 * q + 4, :].rearrange("a r n -> r a n"),
+                )
+
+        def load_sc8(eng):
+            src = w8_scales.bitcast(I32)
+            for q in range(4):
+                eng.dma_start(out=sc8[32 * q + 4 : 32 * q + 12, :].bitcast(I32), in_=src[:, 4 * q : 4 * q + 4, :])
+
+        def load_w4(g0, g1):
+            nc.sync.dma_start(out=w4[:, g0:g1, :].bitcast(I32), in_=w4_words[g0:g1].bitcast(I32).rearrange("a p n -> p a n"))
+
+        def load_w8(g0, g1):
+            src = w8_words[g0:g1].rearrange("a p n i -> p a (n i)").bitcast(I32)
+            nc.sync.dma_start(out=w8[:, g0:g1, :].bitcast(I32), in_=src)
+
+        def relu(eng, s, g, c0, c1):
+            t, base = raw[g, c0]
+            src = t[:, :, c0 - base : c1 - base].rearrange("p j (c i) -> p c j i", i=4)
+            dst = grouped[s, g][:, c0:c1, :].rearrange("p (c i) j -> p c j i", i=4)
+            if eng == "S":
+                nc.scalar.activation(out=dst, in_=src, func=ACT.Relu, bias=zero[:, 0:1], scale=(1.0, -1.0)[s])
+            elif s == 0:
+                nc.vector.tensor_scalar(out=dst, in0=src, scalar1=0.0, scalar2=None, op0=ALU.max)
+            else:
+                nc.vector.tensor_scalar(out=dst, in0=src, scalar1=-1.0, scalar2=0.0, op0=ALU.mult, op1=ALU.max)
+
+        def quant(s, g, c0, c1):
+            nc.vector.quantize_mx(
+                out=codes[s, g][:, c0:c1].bitcast(FP8X4),
+                scales=planes[s, g][:, c0:c1],
+                in_=grouped[s, g][:, c0:c1, :].rearrange("p w j -> p (w j)"),
+            )
+
+        def mm(b, o, m, s, g, c0, c1, start, stop):
+            if s == 0:
+                lhsT = w4[:, g, 256 * m : 256 * (m + 1)].bitcast(FP4X4)
+                lsc = sc4[:, g, 128 * m : 128 * (m + 1)]
+            else:
+                lhsT = w8[:, g, 512 * m : 512 * (m + 1)].bitcast(FP8X4)
+                lsc = sc8[4 * (g + 1) :, 128 * m : 128 * (m + 1)]
+            nc.tensor.matmul_mx(
+                out=acc[b][:, o : o + c1 - c0],
+                lhsT=lhsT,
+                lhsT_scale=lsc,
+                rhs=codes[s, g][:, c0:c1].bitcast(FP8X4),
+                rhs_scale=planes[s, g][:, c0:c1],
+                start=start,
+                stop=stop,
+            )
+
+        def result(c0, c1):
+            res[c0] = keep.tile([P, 4, c1 - c0], F32, name="res%d" % c0, align_bytes=64)
+
+        def evac(eng, b, m, c0, c1):
+            if eng == "S":
+                nc.scalar.copy(out=res[c0][:, m, :], in_=acc[b][:, 0 : c1 - c0])
+            else:
+                nc.vector.tensor_copy(out=res[c0][:, m, :], in_=acc[b][:, 0 : c1 - c0])
+
+        def store(m0, m1, c0, c1):
+            dst = out[128 * m0 : 128 * m1, c0:c1].rearrange("(m p) t -> p m t", p=P)
+            nc.sync.dma_start(out=dst, in_=res[c0][:, m0:m1, :])
+
+        nc.vector.memset(seed[:], 0.0)
+        nc.vector.memset(sc4[:].rearrange("p a n -> p (a n)").bitcast(I32), 0)
+        nc.vector.memset(sc8[:].bitcast(I32), 0)
+        nc.scalar.activation(out=zero[:], in_=seed[:], func=ACT.Relu)
+        load_x(0, 0, 512)
+        load_x(1, 0, 512)
+        load_sc4(nc.sync)
+        load_w4(0, 2)
+        load_x(0, 512, 768)
+        load_sc8(nc.sync)
+        load_w8(0, 1)
+        load_x(0, 768, 1024)
+        load_w8(1, 2)
+        load_x(1, 512, 768)
+        load_x(1, 768, 1024)
+        result(0, 512)
+        result(512, 1024)
+        for g in range(2):
+            relu("V", 0, g, 0, 256)
+            if g == 1:
+                quant(1, 0, 256, 512)
+            relu("V", 0, g, 256, 512)
+            relu("S", 1, g, 0, 256)
+            relu("S", 1, g, 256, 512)
+            quant(0, g, 0, 256)
+            quant(0, g, 256, 512)
+            quant(1, g, 0, 256)
+        quant(1, 1, 256, 512)
+        for g in range(2):
+            for m in range(4):
+                mm(m, 0, m, 0, g, 0, 512, g == 0, False)
+        for g in range(2):
+            for m in range(4):
+                mm(m, 0, m, 1, g, 0, 512, False, g == 1)
+        for c in (512, 768):
+            relu("V", 0, 0, c, c + 256)
+            relu("S", 1, 0, c, c + 256)
+            quant(0, 0, c, c + 256)
+            quant(1, 0, c, c + 256)
+        for s in range(2):
+            for m in range(4):
+                mm(4 + m, 0, m, s, 0, 512, 1024, s == 0, False)
+        evac("S", 0, 0, 0, 512)
+        evac("V", 1, 1, 0, 512)
+        store(0, 2, 0, 512)
+        evac("S", 2, 2, 0, 512)
+        relu("V", 0, 1, 512, 768)
+        relu("S", 1, 1, 512, 768)
+        evac("V", 3, 3, 0, 512)
+        store(2, 4, 0, 512)
+        quant(0, 1, 512, 768)
+        relu("V", 0, 1, 768, 1024)
+        relu("S", 1, 1, 768, 1024)
+        quant(1, 1, 512, 768)
+        quant(0, 1, 768, 1024)
+        quant(1, 1, 768, 1024)
+        for m in range(4):
+            mm(4 + m, 0, m, 0, 1, 512, 1024, False, False)
+            mm(4 + m, 0, m, 1, 1, 512, 1024, False, True)
+            evac("SV"[m % 2], 4 + m, m, 512, 1024)
+            store(m, m + 1, 512, 1024)

@@ -29,7 +29,7 @@ def tile_mix_feat_fm_crelu_none_kernel(tc, x, w4_words, w4_scales, w8_words, w8_
         w4 = keep.tile([P, 2, 2 * M], U8, name="w4", align_bytes=64)
         w8 = keep.tile([P, 2, 4 * M], U8, name="w8", align_bytes=64)
         sc4 = keep.tile([P, 2, M], U8, name="sc4", align_bytes=64)
-        sc8 = keep.tile([P, M], U8, name="sc8", align_bytes=64)
+        sc8 = keep.tile([P, 2, M], U8, name="sc8", align_bytes=64)
         seed = keep.tile([P, 8], F32, name="seed")
         zero = keep.tile([P, 8], F32, name="zero")
         raw, grouped, codes, planes, acc, res = {}, {}, {}, {}, {}, {}
@@ -47,25 +47,22 @@ def tile_mix_feat_fm_crelu_none_kernel(tc, x, w4_words, w4_scales, w8_words, w8_
             for c in range(c0, c1, 32):
                 raw[g, c] = (t, c0)
 
-        def load_sc4(eng):
-            src = w4_scales.bitcast(I32)
-            for q in range(4):
-                eng.dma_start(
-                    out=sc4[32 * q : 32 * q + 4, :, :].bitcast(I32),
-                    in_=src[:, 4 * q : 4 * q + 4, :].rearrange("a r n -> r a n"),
+        def load_sc(s, r0, r1):
+            src = (w4_scales, w8_scales)[s].bitcast(I32)
+            for r in range(r0, r1):
+                nc.sync.dma_start(
+                    out=(sc4, sc8)[s][4 * s + r : P : 32, :, :].bitcast(I32),
+                    in_=src[:, r:16:4, :].rearrange("a q n -> q a n"),
                 )
 
-        def load_sc8(eng):
-            src = w8_scales.bitcast(I32)
-            for q in range(4):
-                eng.dma_start(out=sc8[32 * q + 4 : 32 * q + 12, :].bitcast(I32), in_=src[:, 4 * q : 4 * q + 4, :])
-
-        def load_w4(g0, g1):
-            nc.sync.dma_start(out=w4[:, g0:g1, :].bitcast(I32), in_=w4_words[g0:g1].bitcast(I32).rearrange("a p n -> p a n"))
-
-        def load_w8(g0, g1):
-            src = w8_words[g0:g1].rearrange("a p n i -> p a (n i)").bitcast(I32)
-            nc.sync.dma_start(out=w8[:, g0:g1, :].bitcast(I32), in_=src)
+        def load_w(s, g0, g1, m0=0, m1=4):
+            if s == 0:
+                src = w4_words[g0:g1, :, 256 * m0 : 256 * m1]
+                dst = w4[:, g0:g1, 256 * m0 : 256 * m1]
+            else:
+                src = w8_words[g0:g1].rearrange("a p n i -> a p (n i)")[:, :, 512 * m0 : 512 * m1]
+                dst = w8[:, g0:g1, 512 * m0 : 512 * m1]
+            nc.sync.dma_start(out=dst.bitcast(I32), in_=src.bitcast(I32).rearrange("a p n -> p a n"))
 
         def relu(eng, s, g, c0, c1):
             t, base = raw[g, c0]
@@ -91,7 +88,7 @@ def tile_mix_feat_fm_crelu_none_kernel(tc, x, w4_words, w4_scales, w8_words, w8_
                 lsc = sc4[:, g, 128 * m : 128 * (m + 1)]
             else:
                 lhsT = w8[:, g, 512 * m : 512 * (m + 1)].bitcast(FP8X4)
-                lsc = sc8[4 * (g + 1) :, 128 * m : 128 * (m + 1)]
+                lsc = sc8[4:, g, 128 * m : 128 * (m + 1)]
             nc.tensor.matmul_mx(
                 out=acc[b][:, o : o + c1 - c0],
                 lhsT=lhsT,
@@ -117,62 +114,93 @@ def tile_mix_feat_fm_crelu_none_kernel(tc, x, w4_words, w4_scales, w8_words, w8_
 
         nc.vector.memset(seed[:], 0.0)
         nc.vector.memset(sc4[:].rearrange("p a n -> p (a n)").bitcast(I32), 0)
-        nc.vector.memset(sc8[:].bitcast(I32), 0)
+        nc.vector.memset(sc8[:].rearrange("p a n -> p (a n)").bitcast(I32), 0)
         nc.scalar.activation(out=zero[:], in_=seed[:], func=ACT.Relu)
-        load_x(0, 0, 512)
-        load_x(1, 0, 512)
-        load_sc4(nc.sync)
-        load_w4(0, 2)
+        def unit(g, c0, c1, cut, first=0):
+            relu("V", first, g, c0, c1)
+            relu("S", 1 - first, g, c0, cut)
+            if cut < c1:
+                relu("V", 1 - first, g, cut, c1)
+        def p8(b, c0, g, ms=range(4)):
+            for m in ms:
+                mm(b + m, 0, m, 1, g, c0, c0 + 256, g == 0, g == 1)
+        def p4(b, c0, g, ms=range(4)):
+            for m in ms:
+                mm(b + m, 0, m, 0, g, c0, c0 + 128, False, False)
+                mm(b + m, 128, m, 0, g, c0 + 128, c0 + 256, False, False)
+
+        load_x(0, 0, 256)
+        load_x(0, 256, 512)
+        load_x(1, 0, 256)
+        load_sc(0, 0, 4)
+        load_w(0, 0, 2)
+        load_x(1, 256, 512)
         load_x(0, 512, 768)
-        load_sc8(nc.sync)
-        load_w8(0, 1)
-        load_x(0, 768, 1024)
-        load_w8(1, 2)
+        load_sc(1, 0, 4)
+        load_w(1, 0, 2, 0, 2)
         load_x(1, 512, 768)
+        load_w(1, 0, 2, 2, 4)
+        load_x(0, 768, 1024)
         load_x(1, 768, 1024)
         result(0, 512)
-        result(512, 1024)
-        for g in range(2):
-            relu("V", 0, g, 0, 256)
-            if g == 1:
-                quant(1, 0, 256, 512)
-            relu("V", 0, g, 256, 512)
-            relu("S", 1, g, 0, 256)
-            relu("S", 1, g, 256, 512)
-            quant(0, g, 0, 256)
-            quant(0, g, 256, 512)
-            quant(1, g, 0, 256)
+        result(512, 768)
+        result(768, 1024)
+        unit(0, 0, 256, 256)
+        quant(0, 0, 0, 256)
+        unit(0, 256, 512, 512)
+        quant(1, 0, 0, 256)
+        quant(0, 0, 256, 512)
+        for m in range(4):
+            mm(m, 0, m, 0, 0, 0, 512, True, False)
+        unit(1, 0, 256, 256)
+        quant(1, 0, 256, 512)
+        quant(0, 1, 0, 256)
+        quant(1, 1, 0, 256)
+        unit(1, 256, 512, 512)
+        quant(0, 1, 256, 512)
+        for m in range(3):
+            mm(m, 0, m, 0, 1, 0, 512, False, False)
         quant(1, 1, 256, 512)
-        for g in range(2):
-            for m in range(4):
-                mm(m, 0, m, 0, g, 0, 512, g == 0, False)
-        for g in range(2):
-            for m in range(4):
-                mm(m, 0, m, 1, g, 0, 512, False, g == 1)
-        for c in (512, 768):
-            relu("V", 0, 0, c, c + 256)
-            relu("S", 1, 0, c, c + 256)
-            quant(0, 0, c, c + 256)
-            quant(1, 0, c, c + 256)
-        for s in range(2):
-            for m in range(4):
-                mm(4 + m, 0, m, s, 0, 512, 1024, s == 0, False)
+        for m in range(2):
+            mm(m, 0, m, 1, 0, 0, 512, False, False)
+            mm(m, 0, m, 1, 1, 0, 512, False, True)
+        mm(3, 0, 3, 0, 1, 0, 512, False, False)
+        unit(0, 512, 768, 768, 1)
+        quant(1, 0, 512, 768)
+        quant(0, 0, 512, 768)
+        p8(4, 512, 0, (0, 1))
+        p4(4, 512, 0, (0, 1))
         evac("S", 0, 0, 0, 512)
+        for m in range(2, 4):
+            mm(m, 0, m, 1, 0, 0, 512, False, False)
+            mm(m, 0, m, 1, 1, 0, 512, False, True)
+        unit(1, 512, 768, 704)
+        quant(0, 1, 512, 768)
         evac("V", 1, 1, 0, 512)
         store(0, 2, 0, 512)
-        evac("S", 2, 2, 0, 512)
-        relu("V", 0, 1, 512, 768)
-        relu("S", 1, 1, 512, 768)
-        evac("V", 3, 3, 0, 512)
-        store(2, 4, 0, 512)
-        quant(0, 1, 512, 768)
-        relu("V", 0, 1, 768, 1024)
-        relu("S", 1, 1, 768, 1024)
         quant(1, 1, 512, 768)
+        p8(4, 512, 0, (2, 3))
+        p4(4, 512, 0, (2, 3))
+        for m in range(4):
+            p4(4, 512, 1, (m,))
+            p8(4, 512, 1, (m,))
+        evac("S", 2, 2, 0, 512)
+        unit(0, 768, 1024, 896, 1)
+        evac("S", 3, 3, 0, 512)
+        store(2, 4, 0, 512)
+        quant(1, 0, 768, 1024)
+        quant(0, 0, 768, 1024)
+        unit(1, 768, 1024, 896)
+        p8(0, 768, 0)
+        p4(0, 768, 0)
+        for m in range(4):
+            evac("S", 4 + m, m, 512, 768)
+        store(0, 4, 512, 768)
         quant(0, 1, 768, 1024)
         quant(1, 1, 768, 1024)
         for m in range(4):
-            mm(4 + m, 0, m, 0, 1, 512, 1024, False, False)
-            mm(4 + m, 0, m, 1, 1, 512, 1024, False, True)
-            evac("SV"[m % 2], 4 + m, m, 512, 1024)
-            store(m, m + 1, 512, 1024)
+            p4(0, 768, 1, (m,))
+            p8(0, 768, 1, (m,))
+            evac("VS"[m % 2], m, m, 768, 1024)
+            if m % 2:
+                store(m - 1, m + 1, 768, 1024)

from contextlib import ExitStack

import concourse.mybir as mybir

K, M, T = 1024, 512, 1024
FLOPS = 2 * 2 * K * M * T

F32 = mybir.dt.float32
BF16 = mybir.dt.bfloat16
I32 = mybir.dt.int32
U32 = mybir.dt.uint32
U8 = mybir.dt.uint8
FP8X4 = mybir.dt.float8_e4m3fn_x4
FP4X4 = mybir.dt.float4_e2m1fn_x4
ALU = mybir.AluOpType
ACT = mybir.ActivationFunctionType

P = 128
PACK = 4


def tile_mix_feat_fm_crelu_none_kernel(tc, x, w4_words, w4_scales, w8_words, w8_scales, out):
    nc = tc.nc
    with ExitStack() as ctx:
        keep = ctx.enter_context(tc.tile_pool(name="keep", bufs=1))
        psum = ctx.enter_context(tc.psum_pool(name="psum", bufs=1))
        ctx.enter_context(tc.manual_schedule())

        w4 = keep.tile([P, 2, 2 * M], U8, name="w4", align_bytes=64)
        w8 = keep.tile([P, 2, 4 * M], U8, name="w8", align_bytes=64)
        sc4 = keep.tile([P, 2, M], U8, name="sc4", align_bytes=64)
        sc8 = keep.tile([P, 2, M], U8, name="sc8", align_bytes=64)
        seed = keep.tile([P, 8], F32, name="seed")
        zero = keep.tile([P, 8], F32, name="zero")
        raw, grouped, codes, planes, acc, res = {}, {}, {}, {}, {}, {}
        for g in range(2):
            for s in range(2):
                grouped[s, g] = keep.tile([P, T, PACK], BF16, name="grp%d%d" % (s, g), align_bytes=64)
                codes[s, g] = keep.tile([P, T], U32, name="cod%d%d" % (s, g), align_bytes=64)
                planes[s, g] = keep.tile([P, T], U8, name="pln%d%d" % (s, g), align_bytes=64)
        for b in range(8):
            acc[b] = psum.tile([P, 512], F32, name="acc%d" % b)

        def load_x(g, c0, c1):
            t = keep.tile([P, PACK, c1 - c0], F32, name="raw%d_%d" % (g, c0), align_bytes=64)
            nc.sync.dma_start(out=t[:], in_=x[512 * g : 512 * (g + 1), c0:c1].rearrange("(p j) w -> p j w", j=PACK))
            for c in range(c0, c1, 32):
                raw[g, c] = (t, c0)

        def load_sc(s, r0, r1):
            src = (w4_scales, w8_scales)[s].bitcast(I32)
            for r in range(r0, r1):
                nc.sync.dma_start(
                    out=(sc4, sc8)[s][4 * s + r : P : 32, :, :].bitcast(I32),
                    in_=src[:, r:16:4, :].rearrange("a q n -> q a n"),
                )

        def load_w(s, g0, g1, m0=0, m1=4):
            if s == 0:
                src = w4_words[g0:g1, :, 256 * m0 : 256 * m1]
                dst = w4[:, g0:g1, 256 * m0 : 256 * m1]
            else:
                src = w8_words[g0:g1].rearrange("a p n i -> a p (n i)")[:, :, 512 * m0 : 512 * m1]
                dst = w8[:, g0:g1, 512 * m0 : 512 * m1]
            nc.sync.dma_start(out=dst.bitcast(I32), in_=src.bitcast(I32).rearrange("a p n -> p a n"))

        def relu(eng, s, g, c0, c1):
            t, base = raw[g, c0]
            src = t[:, :, c0 - base : c1 - base].rearrange("p j (c i) -> p c j i", i=4)
            dst = grouped[s, g][:, c0:c1, :].rearrange("p (c i) j -> p c j i", i=4)
            if eng == "S":
                nc.scalar.activation(out=dst, in_=src, func=ACT.Relu, bias=zero[:, 0:1], scale=(1.0, -1.0)[s])
            elif s == 0:
                nc.vector.tensor_scalar(out=dst, in0=src, scalar1=0.0, scalar2=None, op0=ALU.max)
            else:
                nc.vector.tensor_scalar(out=dst, in0=src, scalar1=-1.0, scalar2=0.0, op0=ALU.mult, op1=ALU.max)

        def quant(s, g, c0, c1):
            nc.vector.quantize_mx(
                out=codes[s, g][:, c0:c1].bitcast(FP8X4),
                scales=planes[s, g][:, c0:c1],
                in_=grouped[s, g][:, c0:c1, :].rearrange("p w j -> p (w j)"),
            )

        def mm(b, o, m, s, g, c0, c1, start, stop):
            if s == 0:
                lhsT = w4[:, g, 256 * m : 256 * (m + 1)].bitcast(FP4X4)
                lsc = sc4[:, g, 128 * m : 128 * (m + 1)]
            else:
                lhsT = w8[:, g, 512 * m : 512 * (m + 1)].bitcast(FP8X4)
                lsc = sc8[4:, g, 128 * m : 128 * (m + 1)]
            nc.tensor.matmul_mx(
                out=acc[b][:, o : o + c1 - c0],
                lhsT=lhsT,
                lhsT_scale=lsc,
                rhs=codes[s, g][:, c0:c1].bitcast(FP8X4),
                rhs_scale=planes[s, g][:, c0:c1],
                start=start,
                stop=stop,
            )

        def result(c0, c1):
            res[c0] = keep.tile([P, 4, c1 - c0], F32, name="res%d" % c0, align_bytes=64)

        def evac(eng, b, m, c0, c1):
            if eng == "S":
                nc.scalar.copy(out=res[c0][:, m, :], in_=acc[b][:, 0 : c1 - c0])
            else:
                nc.vector.tensor_copy(out=res[c0][:, m, :], in_=acc[b][:, 0 : c1 - c0])

        def store(m0, m1, c0, c1):
            dst = out[128 * m0 : 128 * m1, c0:c1].rearrange("(m p) t -> p m t", p=P)
            nc.sync.dma_start(out=dst, in_=res[c0][:, m0:m1, :])

        nc.vector.memset(seed[:], 0.0)
        nc.vector.memset(sc4[:].rearrange("p a n -> p (a n)").bitcast(I32), 0)
        nc.vector.memset(sc8[:].rearrange("p a n -> p (a n)").bitcast(I32), 0)
        nc.scalar.activation(out=zero[:], in_=seed[:], func=ACT.Relu)
        def unit(g, c0, c1, cut, first=0):
            relu("V", first, g, c0, c1)
            relu("S", 1 - first, g, c0, cut)
            if cut < c1:
                relu("V", 1 - first, g, cut, c1)
        def p8(b, c0, g, ms=range(4)):
            for m in ms:
                mm(b + m, 0, m, 1, g, c0, c0 + 256, g == 0, g == 1)
        def p4(b, c0, g, ms=range(4)):
            for m in ms:
                mm(b + m, 0, m, 0, g, c0, c0 + 128, False, False)
                mm(b + m, 128, m, 0, g, c0 + 128, c0 + 256, False, False)

        load_x(0, 0, 256)
        load_x(0, 256, 512)
        load_x(1, 0, 256)
        load_sc(0, 0, 4)
        load_w(0, 0, 2)
        load_x(1, 256, 512)
        load_x(0, 512, 768)
        load_sc(1, 0, 4)
        load_w(1, 0, 2, 0, 2)
        load_x(1, 512, 768)
        load_w(1, 0, 2, 2, 4)
        load_x(0, 768, 1024)
        load_x(1, 768, 1024)
        result(0, 512)
        result(512, 768)
        result(768, 1024)
        unit(0, 0, 256, 256)
        quant(0, 0, 0, 256)
        unit(0, 256, 512, 512)
        quant(1, 0, 0, 256)
        quant(0, 0, 256, 512)
        for m in range(4):
            mm(m, 0, m, 0, 0, 0, 512, True, False)
        unit(1, 0, 256, 256)
        quant(1, 0, 256, 512)
        quant(0, 1, 0, 256)
        quant(1, 1, 0, 256)
        unit(1, 256, 512, 512)
        quant(0, 1, 256, 512)
        for m in range(3):
            mm(m, 0, m, 0, 1, 0, 512, False, False)
        quant(1, 1, 256, 512)
        for m in range(2):
            mm(m, 0, m, 1, 0, 0, 512, False, False)
            mm(m, 0, m, 1, 1, 0, 512, False, True)
        mm(3, 0, 3, 0, 1, 0, 512, False, False)
        unit(0, 512, 768, 768, 1)
        quant(1, 0, 512, 768)
        quant(0, 0, 512, 768)
        p8(4, 512, 0, (0, 1))
        p4(4, 512, 0, (0, 1))
        evac("S", 0, 0, 0, 512)
        for m in range(2, 4):
            mm(m, 0, m, 1, 0, 0, 512, False, False)
            mm(m, 0, m, 1, 1, 0, 512, False, True)
        unit(1, 512, 768, 704)
        quant(0, 1, 512, 768)
        evac("V", 1, 1, 0, 512)
        store(0, 2, 0, 512)
        quant(1, 1, 512, 768)
        p8(4, 512, 0, (2, 3))
        p4(4, 512, 0, (2, 3))
        for m in range(4):
            p4(4, 512, 1, (m,))
            p8(4, 512, 1, (m,))
        evac("S", 2, 2, 0, 512)
        unit(0, 768, 1024, 896, 1)
        evac("S", 3, 3, 0, 512)
        store(2, 4, 0, 512)
        quant(1, 0, 768, 1024)
        quant(0, 0, 768, 1024)
        unit(1, 768, 1024, 896)
        p8(0, 768, 0)
        p4(0, 768, 0)
        for m in range(4):
            evac("S", 4 + m, m, 512, 768)
        store(0, 4, 512, 768)
        quant(0, 1, 768, 1024)
        quant(1, 1, 768, 1024)
        for m in range(4):
            p4(0, 768, 1, (m,))
            p8(0, 768, 1, (m,))
            evac("VS"[m % 2], m, m, 768, 1024)
            if m % 2:
                store(m - 1, m + 1, 768, 1024)
